import numpy as np
import ml_dtypes


def mxq(x, axis, fmt="e4m3"):
    dtype, down = {"e4m3": (ml_dtypes.float8_e4m3fn, 7), "e5m2": (ml_dtypes.float8_e5m2, 14)}[fmt]
    v = np.moveaxis(np.asarray(x, np.float32).astype(ml_dtypes.bfloat16).astype(np.float64), axis, -1)
    blocks = v.reshape(v.shape[:-1] + (-1, 32))
    amax = np.abs(blocks).max(-1, keepdims=True)
    byte = np.maximum(np.where(amax > 0, np.frexp(amax)[1] - 1 + 127, 0) - down, 1)
    scale = np.exp2(byte - 127.0)
    codes = (blocks / scale).astype(np.float32).astype(dtype).astype(np.float64)
    return np.moveaxis((codes * scale).reshape(v.shape), -1, axis)


WIDE = False


def mx_kscale(k):
    if not WIDE:
        return np.ones(k)
    levels = np.array([10, -10, 5, -5, 0])
    if k % 512:
        return np.exp2(np.random.permutation(np.resize(levels, k // 32))).repeat(32)
    a = np.empty((k // 512, 16))
    for p in range(k // 512):
        a[p, :8] = np.random.permutation(np.resize(levels, 8))
        for g in range(8):
            far = levels[np.abs(levels - a[p, g]) >= 10]
            a[p, g + 8] = far[np.random.randint(len(far))]
    return np.exp2(a.ravel()).repeat(32)


def f64(x):
    return np.asarray(x).astype(np.float64)


def striped(idx):
    return np.tile(idx.reshape(-1, 16).T, (8, 1)).astype(np.uint16)


def unstriped(offs):
    return offs[:16].T.reshape(-1).astype(np.int64)


def striped8(idx):
    return np.concatenate([x.reshape(-1, 16).T for x in idx]).astype(np.uint16)


def runs(offs, k):
    lists = np.stack([offs[16 * r : 16 * r + 16].T.reshape(-1) for r in range(8)]).astype(np.int64)
    return lists[np.arange(k) % 512 // 64]


def pack_weight(w):
    k, n = w.shape
    w = f64(np.asarray(w, np.float32).astype(ml_dtypes.bfloat16)).reshape(k // 32, 32, n)
    amax = np.abs(w).max(1)
    byte = np.clip(np.where(amax > 0, np.frexp(amax)[1] - 1 + 127 - 7, 1), 1, 254)
    scaled = (w * np.exp2(127.0 - byte)[:, None, :]).reshape(k, n).astype(np.float32)
    words = np.ascontiguousarray(scaled.reshape(k // 512, 128, 4, n).transpose(0, 1, 3, 2)).astype(ml_dtypes.float8_e4m3fn).view(np.uint8)
    return words, np.ascontiguousarray(byte.astype(np.uint8).reshape(k // 512, 16, n))


def unpack_weight(words, scales):
    g, p, n, _ = words.shape
    vals = np.ascontiguousarray(words).view(ml_dtypes.float8_e4m3fn).astype(np.float64) * np.repeat(np.exp2(scales.astype(np.float64) - 127.0), 8, axis=1)[..., None]
    return vals.transpose(0, 1, 3, 2).reshape(g * 512, n)


def sigmoid(v):
    return 1.0 / (1.0 + np.exp(-np.maximum(v, -700.0)))


K, T, S, H, G = 512, 2048, 512, 512, 2048


def setup_inputs():
    n = np.random.standard_normal
    s = mx_kscale(K)[:, None]
    packed_xT = pack_weight(n((K, T)) * s)
    packed_dT = pack_weight(n((K, G)) / s)
    return {
        "x_words": packed_xT[0],
        "x_scales": packed_xT[1],
        "w1": (n((K, H)) / np.sqrt(K) / s).astype(np.float32),
        "gs": (np.random.uniform(0.5, 1.5, (K, 1)) * s).astype(np.float32),
        "d_words": packed_dT[0],
        "d_scales": packed_dT[1],
        "offs": striped(np.random.permutation(T)[:S]),
        "b_x1": striped8(np.stack([np.random.permutation(S) for _ in range(8)])),
        "b_x2": striped8(np.stack([np.random.permutation(S) for _ in range(8)])),
        "b_x3": striped8(np.stack([np.random.permutation(S) for _ in range(8)])),
        "kq": striped8(np.random.randint(0, G, (8, H))),
    }


def reference(x_words, x_scales, w1, gs, d_words, d_scales, offs, b_x1, b_x2, b_x3, kq):
    d_kq = unpack_weight(d_words, d_scales)[np.arange(K)[:, None], runs(kq, K)]
    xq = unpack_weight(x_words, x_scales)[:, unstriped(offs)]
    y = mxq(f64(w1), 0, "e4m3").T @ xq
    x1 = y[np.arange(H)[:, None], runs(b_x1, H)]
    x2 = y[np.arange(H)[:, None], runs(b_x2, H)]
    x3 = y[np.arange(H)[:, None], runs(b_x3, H)]
    mx = np.maximum(np.maximum(x1, x2), x3)
    md = np.maximum(np.minimum(x1, x2), np.minimum(np.maximum(x1, x2), x3))
    z = f64(gs) * ((mx - md) * sigmoid(md))
    return 0.0625 * ((d_kq.T @ mxq(z, 0, "e4m3")))

@@ -1,0 +1,223 @@
+from contextlib import ExitStack
+
+import concourse.mybir as mybir
+
+F32 = mybir.dt.float32
+BF16 = mybir.dt.bfloat16
+I32 = mybir.dt.int32
+U32 = mybir.dt.uint32
+U16 = mybir.dt.uint16
+U8 = mybir.dt.uint8
+FP8X4 = mybir.dt.float8_e4m3fn_x4
+ALU = mybir.AluOpType
+ACT = mybir.ActivationFunctionType
+
+P = 128
+PACK = 4
+K, T, S, H, G = 512, 2048, 512, 512, 2048
+HALF = S // 2
+CHUNKS = ((0, 256), (256, 128), (384, 128))
+FLOPS = 2 * K * H * S + 2 * K * H * S
+
+
+def tile_picked_auction2_none_p_kernel(
+    tc, x_words, x_scales, w1, gs, d_words, d_scales, offs, b_x1, b_x2, b_x3, kq, out
+):
+    nc = tc.nc
+    with ExitStack() as ctx:
+        held = ctx.enter_context(tc.tile_pool(name="held", bufs=1))
+        psum = ctx.enter_context(tc.psum_pool(name="psum", bufs=8))
+
+        def tile(shape, dtype, name):
+            return held.tile(shape, dtype, name=name, align_bytes=64)
+
+        def entries(lst, start, count):
+            return lst[:, start // 16 : (start + count) // 16]
+
+        offs_t = held.tile([P, S // 16], U16, name="offs_t")
+        kq_t = held.tile([P, H // 16], U16, name="kq_t")
+        b1_t = held.tile([P, S // 16], U16, name="b1_t")
+        b2_t = held.tile([P, S // 16], U16, name="b2_t")
+        b3_t = held.tile([P, S // 16], U16, name="b3_t")
+        xs_tab = tile([P, T], U8, "xs_tab")
+        ds_tab = tile([P, G], U8, "ds_tab")
+        xw_tab = tile([P, T], I32, "xw_tab")
+        dw_tab = tile([P, G], I32, "dw_tab")
+        w_raw = tile([P, PACK, H], F32, "w_raw")
+        gs_t = tile([P, PACK], F32, "gs_t")
+        ds_plane = tile([P, H], U8, "ds_plane")
+        warm = tile([P, 2], F32, "warm")
+
+        nc.vector.memset(xs_tab[:].bitcast(I32), 0)
+        nc.vector.memset(ds_tab[:].bitcast(I32), 0)
+        nc.vector.memset(warm[:, 0:1], 0.0)
+        nc.vector.memset(ds_plane[:].bitcast(I32), 0)
+
+        nc.sync.dma_start(offs_t[:], offs)
+        nc.sync.dma_start(w_raw[:], w1.rearrange("(p j) c -> p j c", j=PACK))
+        for q in range(4):
+            nc.sync.dma_start(
+                xs_tab[32 * q : 32 * q + 4, :].bitcast(I32), x_scales[0, 4 * q : 4 * q + 4, :].bitcast(I32)
+            )
+        nc.sync.dma_start(xw_tab[:], x_words[0].rearrange("p n t -> p (n t)").bitcast(I32))
+        nc.sync.dma_start(kq_t[:], kq)
+        nc.sync.dma_start(b1_t[:], b_x1)
+        nc.sync.dma_start(b2_t[:], b_x2)
+        nc.sync.dma_start(b3_t[:], b_x3)
+        nc.sync.dma_start(ds_tab[0:P:8, :].bitcast(I32), d_scales[0].bitcast(I32))
+        nc.sync.dma_start(dw_tab[:], d_words[0].rearrange("p n t -> p (n t)").bitcast(I32))
+        nc.sync.dma_start(gs_t[:], gs.rearrange("(p t) o -> p (t o)", t=PACK))
+
+        nc.scalar.activation(warm[:, 1:2], warm[:, 0:1], ACT.Sigmoid)
+
+
+        w_src = w_raw[:].rearrange("p j (m t) -> p m j t", t=PACK)
+        w_bf = [tile([P, 2, P, PACK], BF16, f"w_bf{g}") for g in range(2)]
+        w_codes = [tile([P, 2 * P], U32, f"w_codes{g}") for g in range(2)]
+        w_scales = [tile([P, 2 * P], U8, f"w_scales{g}") for g in range(2)]
+        nc.vector.tensor_copy(w_bf[0][:].rearrange("p t m j -> p m j t"), w_src[:, :, :, 0:2])
+        nc.scalar.copy(w_bf[1][:].rearrange("p t m j -> p m j t"), w_src[:, :, :, 2:4])
+        xs_pick = tile([P, S], U8, "xs_pick")
+        nc.vector.tensor_copy(xs_pick[:], xs_tab[:].indirect(offs_t[:]))
+        for g in range(2):
+            nc.vector.quantize_mx(
+                out=w_codes[g][:].bitcast(FP8X4), scales=w_scales[g][:], in_=w_bf[g][:].rearrange("p t m j -> p (t m j)")
+            )
+
+        xw_pick = [tile([P, HALF], U32, f"xw_pick{c}") for c in range(2)]
+        y = [tile([P, S], F32, f"y{t}") for t in range(PACK)]
+        for c in range(2):
+            nc.vector.tensor_copy(xw_pick[c][:], xw_tab[:].bitcast(U32).indirect(entries(offs_t, c * HALF, HALF)))
+        ds_pick = tile([P, H], U8, "ds_pick")
+        nc.vector.tensor_copy(ds_pick[:], ds_tab[:].indirect(kq_t[:]))
+        for r in range(4):
+            nc.sync.dma_start(ds_plane[r:P:32, :].bitcast(I32), ds_pick[8 * r : P : 32, :].bitcast(I32))
+        for g, c in ((0, 0), (0, 1), (1, 0), (1, 1)):
+            cols = slice(c * HALF, (c + 1) * HALF)
+            for t in (2 * g, 2 * g + 1):
+                bank = psum.tile([P, 512], F32, name="bank")
+                m_cols = slice((t % 2) * P, (t % 2 + 1) * P)
+                nc.tensor.matmul_mx(
+                    bank[:, :HALF],
+                    lhsT=w_codes[t // 2][:, m_cols].bitcast(FP8X4),
+                    lhsT_scale=w_scales[t // 2][:, m_cols],
+                    rhs=xw_pick[c][:].bitcast(FP8X4),
+                    rhs_scale=xs_pick[:, cols],
+                    start=True,
+                    stop=True,
+                )
+                nc.scalar.copy(y[t][:, cols], bank[:, :HALF])
+
+        dw_pick = tile([P, H], U32, "dw_pick")
+
+        def chunk_tiles(c):
+            n = CHUNKS[c][1]
+            names = ("a", "p", "ap", "h", "w", "u", "au", "nmd", "s", "z", "o")
+            d = {name: tile([P, PACK, n], F32, f"{name}{c}") for name in names}
+            d["zb"] = tile([P, n, PACK], BF16, f"zb{c}")
+            d["zq"] = tile([P, n], U32, f"zq{c}")
+            d["zs"] = tile([P, n], U8, f"zs{c}")
+            return d
+
+        tl = [chunk_tiles(c) for c in range(len(CHUNKS))]
+        pairs = (slice(0, 2), slice(2, 4))
+
+        def first_two(c):
+            d = tl[c]
+            j0, n = CHUNKS[c]
+            for g in pairs:
+                for t in range(g.start, g.stop):
+                    nc.vector.tensor_copy(d["a"][:, t, :], y[t][:].indirect(entries(b1_t, j0, n)))
+                for t in range(g.start, g.stop):
+                    nc.vector.tensor_tensor(
+                        d["p"][:, t, :], y[t][:].indirect(entries(b2_t, j0, n)), d["a"][:, t, :], ALU.subtract
+                    )
+                nc.scalar.activation(d["ap"][:, g, :], d["p"][:, g, :], ACT.Abs)
+
+        def larger(c):
+            d = tl[c]
+            for g in pairs:
+                nc.vector.scalar_tensor_tensor(d["h"][:, g, :], d["p"][:, g, :], 0.0, d["a"][:, g, :], ALU.max, ALU.add)
+
+        def third(c):
+            d = tl[c]
+            j0, n = CHUNKS[c]
+            for t in range(PACK):
+                nc.vector.tensor_tensor(
+                    d["w"][:, t, :], y[t][:].indirect(entries(b3_t, j0, n)), d["h"][:, t, :], ALU.subtract
+                )
+
+        def middle(c):
+            d = tl[c]
+            for g in pairs:
+                nc.vector.scalar_tensor_tensor(d["u"][:, g, :], d["w"][:, g, :], -1.0, d["ap"][:, g, :], ALU.mult, ALU.min)
+            for g in pairs:
+                nc.vector.scalar_tensor_tensor(
+                    d["nmd"][:, g, :], d["u"][:, g, :], 0.0, d["h"][:, g, :], ALU.max, ALU.subtract
+                )
+            for g in pairs:
+                nc.scalar.activation(d["au"][:, g, :], d["u"][:, g, :], ACT.Abs)
+            for g in pairs:
+                nc.scalar.activation(d["s"][:, g, :], d["nmd"][:, g, :], ACT.Sigmoid, scale=-1.0)
+
+        def gain(c):
+            d = tl[c]
+            for t in range(PACK):
+                nc.vector.scalar_tensor_tensor(
+                    d["z"][:, t, :], d["au"][:, t, :], gs_t[:, t : t + 1], d["s"][:, t, :], ALU.mult, ALU.mult
+                )
+            src = d["z"][:].rearrange("p t j -> p j t")
+            if c == len(CHUNKS) - 1:
+                nc.vector.tensor_copy(d["zb"][:], src)
+            else:
+                nc.scalar.copy(d["zb"][:], src)
+
+        def product(c):
+            d = tl[c]
+            j0, n = CHUNKS[c]
+            nc.vector.quantize_mx(
+                out=d["zq"][:].bitcast(FP8X4), scales=d["zs"][:], in_=d["zb"][:].rearrange("p j t -> p (j t)")
+            )
+            for gi, g in enumerate(pairs):
+                bank = psum.tile([P, 512], F32, name="bank")
+                for e in range(2):
+                    rows = slice((2 * gi + e) * P, (2 * gi + e + 1) * P)
+                    nc.tensor.matmul_mx(
+                        bank[:, e * n : (e + 1) * n],
+                        lhsT=dw_pick[:, rows].bitcast(FP8X4),
+                        lhsT_scale=ds_plane[:, rows],
+                        rhs=d["zq"][:].bitcast(FP8X4),
+                        rhs_scale=d["zs"][:],
+                        start=True,
+                        stop=True,
+                    )
+                dst = d["o"][:, g, :].rearrange("p a j -> p (a j)")
+                last = c == len(CHUNKS) - 1
+                if last and gi == 1:
+                    nc.vector.tensor_scalar(dst, bank[:, : 2 * n], 0.0625, None, ALU.mult)
+                else:
+                    nc.scalar.activation(dst, bank[:, : 2 * n], ACT.Copy, scale=0.0625)
+                queue = nc.scalar if last and gi == 0 else nc.sync
+                queue.dma_start(
+                    out[2 * gi * P : (2 * gi + 2) * P, j0 : j0 + n].rearrange("(a p) j -> p a j", p=P), d["o"][:, g, :]
+                )
+
+        first_two(0)
+        larger(0)
+        third(0)
+        middle(0)
+        first_two(1)
+        gain(0)
+        larger(1)
+        nc.vector.tensor_copy(dw_pick[:], dw_tab[:].bitcast(U32).indirect(kq_t[:]))
+        third(1)
+        product(0)
+        middle(1)
+        first_two(2)
+        gain(1)
+        larger(2)
+        third(2)
+        product(1)
+        middle(2)
+        gain(2)
+        product(2)

@@ -1,6 +1,7 @@
 from contextlib import ExitStack
 
 import concourse.mybir as mybir
+from concourse.masks import make_identity
 
 F32 = mybir.dt.float32
 BF16 = mybir.dt.bfloat16
@@ -17,6 +18,7 @@ PACK = 4
 K, T, S, H, G = 512, 2048, 512, 512, 2048
 HALF = S // 2
 CHUNKS = ((0, 256), (256, 128), (384, 128))
+REUSE = {("a", 2): "au0", ("w", 2): "zb0", ("u", 2): "au1"}
 FLOPS = 2 * K * H * S + 2 * K * H * S
 
 
@@ -28,8 +30,8 @@ def tile_picked_auction2_none_p_kernel(
         held = ctx.enter_context(tc.tile_pool(name="held", bufs=1))
         psum = ctx.enter_context(tc.psum_pool(name="psum", bufs=8))
 
-        def tile(shape, dtype, name):
-            return held.tile(shape, dtype, name=name, align_bytes=64)
+        def tile(shape, dtype, name, tag=None):
+            return held.tile(shape, dtype, name=name, tag=tag or name, align_bytes=64)
 
         def entries(lst, start, count):
             return lst[:, start // 16 : (start + count) // 16]
@@ -53,8 +55,11 @@ def tile_picked_auction2_none_p_kernel(
         nc.vector.memset(warm[:, 0:1], 0.0)
         nc.vector.memset(ds_plane[:].bitcast(I32), 0)
 
-        nc.sync.dma_start(offs_t[:], offs)
+        ident = tile([P, P], F32, "ident")
+        make_identity(nc, ident[:])
+
         nc.sync.dma_start(w_raw[:], w1.rearrange("(p j) c -> p j c", j=PACK))
+        nc.sync.dma_start(offs_t[:], offs)
         for q in range(4):
             nc.sync.dma_start(
                 xs_tab[32 * q : 32 * q + 4, :].bitcast(I32), x_scales[0, 4 * q : 4 * q + 4, :].bitcast(I32)
@@ -106,14 +111,14 @@ def tile_picked_auction2_none_p_kernel(
                     start=True,
                     stop=True,
                 )
-                nc.scalar.copy(y[t][:, cols], bank[:, :HALF])
+                nc.scalar.activation(y[t][:, cols], bank[:, :HALF], ACT.Copy, scale=-1.0)
 
         dw_pick = tile([P, H], U32, "dw_pick")
 
         def chunk_tiles(c):
             n = CHUNKS[c][1]
-            names = ("a", "p", "ap", "h", "w", "u", "au", "nmd", "s", "z", "o")
-            d = {name: tile([P, PACK, n], F32, f"{name}{c}") for name in names}
+            names = ("a", "p", "ap", "nh", "w", "u", "au", "ru", "z", "o")
+            d = {name: tile([P, PACK, n], F32, f"{name}{c}") for name in names if (name, c) not in REUSE}
             d["zb"] = tile([P, n, PACK], BF16, f"zb{c}")
             d["zq"] = tile([P, n], U32, f"zq{c}")
             d["zs"] = tile([P, n], U8, f"zs{c}")
@@ -121,8 +126,14 @@ def tile_picked_auction2_none_p_kernel(
 
         tl = [chunk_tiles(c) for c in range(len(CHUNKS))]
         pairs = (slice(0, 2), slice(2, 4))
+        last = len(CHUNKS) - 1
+
+        def late(c, name):
+            if (name, c) in REUSE:
+                tl[c][name] = tile([P, PACK, CHUNKS[c][1]], F32, f"{name}{c}", REUSE[name, c])
 
         def first_two(c):
+            late(c, "a")
             d = tl[c]
             j0, n = CHUNKS[c]
             for g in pairs:
@@ -137,37 +148,78 @@ def tile_picked_auction2_none_p_kernel(
         def larger(c):
             d = tl[c]
             for g in pairs:
-                nc.vector.scalar_tensor_tensor(d["h"][:, g, :], d["p"][:, g, :], 0.0, d["a"][:, g, :], ALU.max, ALU.add)
+                nc.vector.scalar_tensor_tensor(d["nh"][:, g, :], d["p"][:, g, :], 0.0, d["a"][:, g, :], ALU.min, ALU.add)
 
         def third(c):
+            late(c, "w")
             d = tl[c]
             j0, n = CHUNKS[c]
             for t in range(PACK):
                 nc.vector.tensor_tensor(
-                    d["w"][:, t, :], y[t][:].indirect(entries(b3_t, j0, n)), d["h"][:, t, :], ALU.subtract
+                    d["w"][:, t, :], y[t][:].indirect(entries(b3_t, j0, n)), d["nh"][:, t, :], ALU.subtract
                 )
 
-        def middle(c):
+        def signed_gain(c):
+            late(c, "u")
             d = tl[c]
             for g in pairs:
-                nc.vector.scalar_tensor_tensor(d["u"][:, g, :], d["w"][:, g, :], -1.0, d["ap"][:, g, :], ALU.mult, ALU.min)
+                nc.vector.tensor_tensor(d["u"][:, g, :], d["w"][:, g, :], d["ap"][:, g, :], ALU.min)
+
+        def price_turned(c):
+            d = tl[c]
+            n = CHUNKS[c][1]
             for g in pairs:
-                nc.vector.scalar_tensor_tensor(
-                    d["nmd"][:, g, :], d["u"][:, g, :], 0.0, d["h"][:, g, :], ALU.max, ALU.subtract
-                )
+                nc.scalar.activation(d["ru"][:, g, :], d["u"][:, g, :], ACT.Relu)
+            turned = []
+            for b in range(n // P):
+                bank = psum.tile([P, 512], F32, name="bank")
+                for t in range(PACK):
+                    for i, name in enumerate(("nh", "ru")):
+                        nc.tensor.matmul(
+                            bank[:, t * P : (t + 1) * P],
+                            lhsT=d[name][:, t, b * P : (b + 1) * P],
+                            rhs=ident[:],
+                            is_transpose=True,
+                            start=i == 0,
+                            stop=i == 1,
+                        )
+                s_t = tile([P, 512], F32, f"s_t{c}_{b}")
+                nc.scalar.activation(s_t[:], bank[:], ACT.Sigmoid, scale=-1.0)
+                turned.append(s_t)
             for g in pairs:
                 nc.scalar.activation(d["au"][:, g, :], d["u"][:, g, :], ACT.Abs)
+            per_bank = 512 // n
+            d["s"] = []
+            for t0 in range(0, PACK, per_bank):
+                bank = psum.tile([P, 512], F32, name="bank")
+                for t in range(t0, t0 + per_bank):
+                    for b in range(n // P):
+                        col = (t - t0) * n + b * P
+                        nc.tensor.transpose(bank[:, col : col + P], turned[b][:, t * P : (t + 1) * P], ident[:])
+                    d["s"].append(bank[:, (t - t0) * n : (t - t0 + 1) * n])
+
+        def price_direct(c):
+            d = tl[c]
+            n = CHUNKS[c][1]
+            nmd = tile([P, PACK, n], F32, "nmd")
+            s = tile([P, PACK, n], F32, "s")
+            nc.scalar.activation(d["au"][:], d["u"][:], ACT.Abs)
             for g in pairs:
-                nc.scalar.activation(d["s"][:, g, :], d["nmd"][:, g, :], ACT.Sigmoid, scale=-1.0)
+                nc.vector.scalar_tensor_tensor(nmd[:, g, :], d["u"][:, g, :], 0.0, d["nh"][:, g, :], ALU.max, ALU.add)
+                nc.scalar.activation(s[:, g, :], nmd[:, g, :], ACT.Sigmoid, scale=-1.0)
+            d["s"] = [s[:, t, :] for t in range(PACK)]
 
         def gain(c):
             d = tl[c]
             for t in range(PACK):
                 nc.vector.scalar_tensor_tensor(
-                    d["z"][:, t, :], d["au"][:, t, :], gs_t[:, t : t + 1], d["s"][:, t, :], ALU.mult, ALU.mult
+                    d["z"][:, t, :], d["au"][:, t, :], gs_t[:, t : t + 1], d["s"][t], ALU.mult, ALU.mult
                 )
+
+        def weave(c):
+            d = tl[c]
             src = d["z"][:].rearrange("p t j -> p j t")
-            if c == len(CHUNKS) - 1:
+            if c > 0:
                 nc.vector.tensor_copy(d["zb"][:], src)
             else:
                 nc.scalar.copy(d["zb"][:], src)
@@ -192,12 +244,11 @@ def tile_picked_auction2_none_p_kernel(
                         stop=True,
                     )
                 dst = d["o"][:, g, :].rearrange("p a j -> p (a j)")
-                last = c == len(CHUNKS) - 1
-                if last and gi == 1:
+                if c == last and gi == 1:
                     nc.vector.tensor_scalar(dst, bank[:, : 2 * n], 0.0625, None, ALU.mult)
                 else:
                     nc.scalar.activation(dst, bank[:, : 2 * n], ACT.Copy, scale=0.0625)
-                queue = nc.scalar if last and gi == 0 else nc.sync
+                queue = nc.scalar if c == last and gi == 0 else nc.sync
                 queue.dma_start(
                     out[2 * gi * P : (2 * gi + 2) * P, j0 : j0 + n].rearrange("(a p) j -> p a j", p=P), d["o"][:, g, :]
                 )
@@ -205,19 +256,25 @@ def tile_picked_auction2_none_p_kernel(
         first_two(0)
         larger(0)
         third(0)
-        middle(0)
-        first_two(1)
-        gain(0)
-        larger(1)
+        signed_gain(0)
+        price_turned(0)
         nc.vector.tensor_copy(dw_pick[:], dw_tab[:].bitcast(U32).indirect(kq_t[:]))
+        first_two(1)
+        larger(1)
         third(1)
-        product(0)
-        middle(1)
+        signed_gain(1)
+        price_turned(1)
+        gain(0)
+        weave(0)
         first_two(2)
-        gain(1)
         larger(2)
+        product(0)
         third(2)
+        gain(1)
+        signed_gain(2)
+        price_direct(2)
+        weave(1)
         product(1)
-        middle(2)
         gain(2)
+        weave(2)
         product(2)

@@ -64,37 +64,44 @@ def tile_picked_auction2_none_p_kernel(
             nc.sync.dma_start(
                 xs_tab[32 * q : 32 * q + 4, :].bitcast(I32), x_scales[0, 4 * q : 4 * q + 4, :].bitcast(I32)
             )
-        nc.sync.dma_start(xw_tab[:], x_words[0].rearrange("p n t -> p (n t)").bitcast(I32))
         nc.sync.dma_start(kq_t[:], kq)
+        nc.gpsimd.dma_start(ds_tab[0:P:8, :].bitcast(I32), d_scales[0].bitcast(I32))
+        nc.sync.dma_start(xw_tab[:], x_words[0].rearrange("p n t -> p (n t)").bitcast(I32))
         nc.sync.dma_start(b1_t[:], b_x1)
         nc.sync.dma_start(b2_t[:], b_x2)
         nc.sync.dma_start(b3_t[:], b_x3)
-        nc.sync.dma_start(ds_tab[0:P:8, :].bitcast(I32), d_scales[0].bitcast(I32))
         nc.sync.dma_start(dw_tab[:], d_words[0].rearrange("p n t -> p (n t)").bitcast(I32))
         nc.sync.dma_start(gs_t[:], gs.rearrange("(p t) o -> p (t o)", t=PACK))
 
         nc.scalar.activation(warm[:, 1:2], warm[:, 0:1], ACT.Sigmoid)
 
 
+        xs_pick = tile([P, S], U8, "xs_pick")
+        nc.vector.tensor_copy(xs_pick[:], xs_tab[:].indirect(offs_t[:]))
+
         w_src = w_raw[:].rearrange("p j (m t) -> p m j t", t=PACK)
         w_bf = [tile([P, 2, P, PACK], BF16, f"w_bf{g}") for g in range(2)]
         w_codes = [tile([P, 2 * P], U32, f"w_codes{g}") for g in range(2)]
         w_scales = [tile([P, 2 * P], U8, f"w_scales{g}") for g in range(2)]
-        nc.vector.tensor_copy(w_bf[0][:].rearrange("p t m j -> p m j t"), w_src[:, :, :, 0:2])
-        nc.scalar.copy(w_bf[1][:].rearrange("p t m j -> p m j t"), w_src[:, :, :, 2:4])
-        xs_pick = tile([P, S], U8, "xs_pick")
-        nc.vector.tensor_copy(xs_pick[:], xs_tab[:].indirect(offs_t[:]))
         for g in range(2):
+            nc.scalar.copy(w_bf[g][:].rearrange("p t m j -> p m j t"), w_src[:, :, :, 2 * g : 2 * g + 2])
+
+        xw_pick = [tile([P, HALF], U32, f"xw_pick{c}") for c in range(2)]
+        ds_pick = tile([P, H], U8, "ds_pick")
+        y = [tile([P, S], F32, f"y{t}") for t in range(PACK)]
+
+        def quantize_w(g):
             nc.vector.quantize_mx(
                 out=w_codes[g][:].bitcast(FP8X4), scales=w_scales[g][:], in_=w_bf[g][:].rearrange("p t m j -> p (t m j)")
             )
 
-        xw_pick = [tile([P, HALF], U32, f"xw_pick{c}") for c in range(2)]
-        y = [tile([P, S], F32, f"y{t}") for t in range(PACK)]
+        quantize_w(0)
+        nc.vector.tensor_copy(ds_pick[:], ds_tab[:].indirect(kq_t[:]))
+        quantize_w(1)
         for c in range(2):
             nc.vector.tensor_copy(xw_pick[c][:], xw_tab[:].bitcast(U32).indirect(entries(offs_t, c * HALF, HALF)))
-        ds_pick = tile([P, H], U8, "ds_pick")
-        nc.vector.tensor_copy(ds_pick[:], ds_tab[:].indirect(kq_t[:]))
+        dw_pick = tile([P, H], U32, "dw_pick")
+        nc.vector.tensor_copy(dw_pick[:], dw_tab[:].bitcast(U32).indirect(kq_t[:]))
         for r in range(4):
             nc.sync.dma_start(ds_plane[r:P:32, :].bitcast(I32), ds_pick[8 * r : P : 32, :].bitcast(I32))
         for g, c in ((0, 0), (0, 1), (1, 0), (1, 1)):
@@ -113,14 +120,11 @@ def tile_picked_auction2_none_p_kernel(
                 )
                 nc.scalar.activation(y[t][:, cols], bank[:, :HALF], ACT.Copy, scale=-1.0)
 
-        dw_pick = tile([P, H], U32, "dw_pick")
-
         def chunk_tiles(c):
             n = CHUNKS[c][1]
             names = ("a", "p", "ap", "nh", "w", "u", "au", "ru", "z", "o")
             d = {name: tile([P, PACK, n], F32, f"{name}{c}") for name in names if (name, c) not in REUSE}
             d["zb"] = tile([P, n, PACK], BF16, f"zb{c}")
-            d["zq"] = tile([P, n], U32, f"zq{c}")
             d["zs"] = tile([P, n], U8, f"zs{c}")
             return d
 
@@ -168,46 +172,46 @@ def tile_picked_auction2_none_p_kernel(
         def price_turned(c):
             d = tl[c]
             n = CHUNKS[c][1]
+            per_bank = 512 // n
+            groups = [slice(t0, t0 + per_bank) for t0 in range(0, PACK, per_bank)]
             for g in pairs:
                 nc.scalar.activation(d["ru"][:, g, :], d["u"][:, g, :], ACT.Relu)
             turned = []
-            for b in range(n // P):
+            for g in groups:
                 bank = psum.tile([P, 512], F32, name="bank")
-                for t in range(PACK):
-                    for i, name in enumerate(("nh", "ru")):
+                terms = [d[name][:, g, :].rearrange("p t j -> p (t j)") for name in ("nh", "ru")]
+                for col in range(0, 512, P):
+                    for i, term in enumerate(terms):
                         nc.tensor.matmul(
-                            bank[:, t * P : (t + 1) * P],
-                            lhsT=d[name][:, t, b * P : (b + 1) * P],
+                            bank[:, col : col + P],
+                            lhsT=term[:, col : col + P],
                             rhs=ident[:],
                             is_transpose=True,
                             start=i == 0,
                             stop=i == 1,
                         )
-                s_t = tile([P, 512], F32, f"s_t{c}_{b}")
+                s_t = tile([P, 512], F32, f"s_t{c}_{g.start}")
                 nc.scalar.activation(s_t[:], bank[:], ACT.Sigmoid, scale=-1.0)
                 turned.append(s_t)
             for g in pairs:
                 nc.scalar.activation(d["au"][:, g, :], d["u"][:, g, :], ACT.Abs)
-            per_bank = 512 // n
             d["s"] = []
-            for t0 in range(0, PACK, per_bank):
+            for s_t in turned:
                 bank = psum.tile([P, 512], F32, name="bank")
-                for t in range(t0, t0 + per_bank):
-                    for b in range(n // P):
-                        col = (t - t0) * n + b * P
-                        nc.tensor.transpose(bank[:, col : col + P], turned[b][:, t * P : (t + 1) * P], ident[:])
-                    d["s"].append(bank[:, (t - t0) * n : (t - t0 + 1) * n])
+                for col in range(0, 512, P):
+                    nc.tensor.transpose(bank[:, col : col + P], s_t[:, col : col + P], ident[:])
+                d["s"].extend(bank[:, i * n : (i + 1) * n] for i in range(per_bank))
 
         def price_direct(c):
             d = tl[c]
             n = CHUNKS[c][1]
             nmd = tile([P, PACK, n], F32, "nmd")
-            s = tile([P, PACK, n], F32, "s")
+            s = [tile([P, 2, n], F32, f"s{gi}") for gi in range(2)]
             nc.scalar.activation(d["au"][:], d["u"][:], ACT.Abs)
-            for g in pairs:
+            for gi, g in enumerate(pairs):
                 nc.vector.scalar_tensor_tensor(nmd[:, g, :], d["u"][:, g, :], 0.0, d["nh"][:, g, :], ALU.max, ALU.add)
-                nc.scalar.activation(s[:, g, :], nmd[:, g, :], ACT.Sigmoid, scale=-1.0)
-            d["s"] = [s[:, t, :] for t in range(PACK)]
+                nc.scalar.activation(s[gi][:], nmd[:, g, :], ACT.Sigmoid, scale=-1.0)
+            d["s"] = [s[t // 2][:, t % 2, :] for t in range(PACK)]
 
         def gain(c):
             d = tl[c]
@@ -219,7 +223,10 @@ def tile_picked_auction2_none_p_kernel(
         def weave(c):
             d = tl[c]
             src = d["z"][:].rearrange("p t j -> p j t")
-            if c > 0:
+            if c == last:
+                for cols in (slice(0, 64), slice(64, 128)):
+                    nc.vector.tensor_copy(d["zb"][:, cols, :], src[:, cols, :])
+            elif c > 0:
                 nc.vector.tensor_copy(d["zb"][:], src)
             else:
                 nc.scalar.copy(d["zb"][:], src)
@@ -227,9 +234,13 @@ def tile_picked_auction2_none_p_kernel(
         def product(c):
             d = tl[c]
             j0, n = CHUNKS[c]
-            nc.vector.quantize_mx(
-                out=d["zq"][:].bitcast(FP8X4), scales=d["zs"][:], in_=d["zb"][:].rearrange("p j t -> p (j t)")
-            )
+            d["zq"] = tile([P, n], U32, f"zq{c}", "s0" if c == last - 1 else None)
+            for cols in (slice(0, 64), slice(64, 128)) if c == last else (slice(0, n),):
+                nc.vector.quantize_mx(
+                    out=d["zq"][:, cols].bitcast(FP8X4),
+                    scales=d["zs"][:, cols],
+                    in_=d["zb"][:, cols, :].rearrange("p j t -> p (j t)"),
+                )
             for gi, g in enumerate(pairs):
                 bank = psum.tile([P, 512], F32, name="bank")
                 for e in range(2):
@@ -258,7 +269,6 @@ def tile_picked_auction2_none_p_kernel(
         third(0)
         signed_gain(0)
         price_turned(0)
-        nc.vector.tensor_copy(dw_pick[:], dw_tab[:].bitcast(U32).indirect(kq_t[:]))
         first_two(1)
         larger(1)
         third(1)
@@ -274,7 +284,7 @@ def tile_picked_auction2_none_p_kernel(
         signed_gain(2)
         price_direct(2)
         weave(1)
-        product(1)
         gain(2)
+        product(1)
         weave(2)
         product(2)

from contextlib import ExitStack

import concourse.mybir as mybir
from concourse.masks import make_identity

F32 = mybir.dt.float32
BF16 = mybir.dt.bfloat16
I32 = mybir.dt.int32
U32 = mybir.dt.uint32
U16 = mybir.dt.uint16
U8 = mybir.dt.uint8
FP8X4 = mybir.dt.float8_e4m3fn_x4
ALU = mybir.AluOpType
ACT = mybir.ActivationFunctionType

P = 128
PACK = 4
K, T, S, H, G = 512, 2048, 512, 512, 2048
HALF = S // 2
CHUNKS = ((0, 256), (256, 128), (384, 128))
REUSE = {("a", 2): "au0", ("w", 2): "zb0", ("u", 2): "au1"}
FLOPS = 2 * K * H * S + 2 * K * H * S


def tile_picked_auction2_none_p_kernel(
    tc, x_words, x_scales, w1, gs, d_words, d_scales, offs, b_x1, b_x2, b_x3, kq, out
):
    nc = tc.nc
    with ExitStack() as ctx:
        held = ctx.enter_context(tc.tile_pool(name="held", bufs=1))
        psum = ctx.enter_context(tc.psum_pool(name="psum", bufs=8))

        def tile(shape, dtype, name, tag=None):
            return held.tile(shape, dtype, name=name, tag=tag or name, align_bytes=64)

        def entries(lst, start, count):
            return lst[:, start // 16 : (start + count) // 16]

        offs_t = held.tile([P, S // 16], U16, name="offs_t")
        kq_t = held.tile([P, H // 16], U16, name="kq_t")
        b1_t = held.tile([P, S // 16], U16, name="b1_t")
        b2_t = held.tile([P, S // 16], U16, name="b2_t")
        b3_t = held.tile([P, S // 16], U16, name="b3_t")
        xs_tab = tile([P, T], U8, "xs_tab")
        ds_tab = tile([P, G], U8, "ds_tab")
        xw_tab = tile([P, T], I32, "xw_tab")
        dw_tab = tile([P, G], I32, "dw_tab")
        w_raw = tile([P, PACK, H], F32, "w_raw")
        gs_t = tile([P, PACK], F32, "gs_t")
        ds_plane = tile([P, H], U8, "ds_plane")
        warm = tile([P, 2], F32, "warm")

        nc.vector.memset(xs_tab[:].bitcast(I32), 0)
        nc.vector.memset(ds_tab[:].bitcast(I32), 0)
        nc.vector.memset(warm[:, 0:1], 0.0)
        nc.vector.memset(ds_plane[:].bitcast(I32), 0)

        ident = tile([P, P], F32, "ident")
        make_identity(nc, ident[:])

        nc.sync.dma_start(w_raw[:], w1.rearrange("(p j) c -> p j c", j=PACK))
        nc.sync.dma_start(offs_t[:], offs)
        for q in range(4):
            nc.sync.dma_start(
                xs_tab[32 * q : 32 * q + 4, :].bitcast(I32), x_scales[0, 4 * q : 4 * q + 4, :].bitcast(I32)
            )
        nc.sync.dma_start(kq_t[:], kq)
        nc.gpsimd.dma_start(ds_tab[0:P:8, :].bitcast(I32), d_scales[0].bitcast(I32))
        nc.sync.dma_start(xw_tab[:], x_words[0].rearrange("p n t -> p (n t)").bitcast(I32))
        nc.sync.dma_start(b1_t[:], b_x1)
        nc.sync.dma_start(b2_t[:], b_x2)
        nc.sync.dma_start(b3_t[:], b_x3)
        nc.sync.dma_start(dw_tab[:], d_words[0].rearrange("p n t -> p (n t)").bitcast(I32))
        nc.sync.dma_start(gs_t[:], gs.rearrange("(p t) o -> p (t o)", t=PACK))

        nc.scalar.activation(warm[:, 1:2], warm[:, 0:1], ACT.Sigmoid)


        xs_pick = tile([P, S], U8, "xs_pick")
        nc.vector.tensor_copy(xs_pick[:], xs_tab[:].indirect(offs_t[:]))

        w_src = w_raw[:].rearrange("p j (m t) -> p m j t", t=PACK)
        w_bf = [tile([P, 2, P, PACK], BF16, f"w_bf{g}") for g in range(2)]
        w_codes = [tile([P, 2 * P], U32, f"w_codes{g}") for g in range(2)]
        w_scales = [tile([P, 2 * P], U8, f"w_scales{g}") for g in range(2)]
        for g in range(2):
            nc.scalar.copy(w_bf[g][:].rearrange("p t m j -> p m j t"), w_src[:, :, :, 2 * g : 2 * g + 2])

        xw_pick = [tile([P, HALF], U32, f"xw_pick{c}") for c in range(2)]
        ds_pick = tile([P, H], U8, "ds_pick")
        y = [tile([P, S], F32, f"y{t}") for t in range(PACK)]

        def quantize_w(g):
            nc.vector.quantize_mx(
                out=w_codes[g][:].bitcast(FP8X4), scales=w_scales[g][:], in_=w_bf[g][:].rearrange("p t m j -> p (t m j)")
            )

        quantize_w(0)
        nc.vector.tensor_copy(ds_pick[:], ds_tab[:].indirect(kq_t[:]))
        quantize_w(1)
        for c in range(2):
            nc.vector.tensor_copy(xw_pick[c][:], xw_tab[:].bitcast(U32).indirect(entries(offs_t, c * HALF, HALF)))
        dw_pick = tile([P, H], U32, "dw_pick")
        nc.vector.tensor_copy(dw_pick[:], dw_tab[:].bitcast(U32).indirect(kq_t[:]))
        for r in range(4):
            nc.sync.dma_start(ds_plane[r:P:32, :].bitcast(I32), ds_pick[8 * r : P : 32, :].bitcast(I32))
        for g, c in ((0, 0), (0, 1), (1, 0), (1, 1)):
            cols = slice(c * HALF, (c + 1) * HALF)
            for t in (2 * g, 2 * g + 1):
                bank = psum.tile([P, 512], F32, name="bank")
                m_cols = slice((t % 2) * P, (t % 2 + 1) * P)
                nc.tensor.matmul_mx(
                    bank[:, :HALF],
                    lhsT=w_codes[t // 2][:, m_cols].bitcast(FP8X4),
                    lhsT_scale=w_scales[t // 2][:, m_cols],
                    rhs=xw_pick[c][:].bitcast(FP8X4),
                    rhs_scale=xs_pick[:, cols],
                    start=True,
                    stop=True,
                )
                nc.scalar.activation(y[t][:, cols], bank[:, :HALF], ACT.Copy, scale=-1.0)

        def chunk_tiles(c):
            n = CHUNKS[c][1]
            names = ("a", "p", "ap", "nh", "w", "u", "au", "ru", "z", "o")
            d = {name: tile([P, PACK, n], F32, f"{name}{c}") for name in names if (name, c) not in REUSE}
            d["zb"] = tile([P, n, PACK], BF16, f"zb{c}")
            d["zs"] = tile([P, n], U8, f"zs{c}")
            return d

        tl = [chunk_tiles(c) for c in range(len(CHUNKS))]
        pairs = (slice(0, 2), slice(2, 4))
        last = len(CHUNKS) - 1

        def late(c, name):
            if (name, c) in REUSE:
                tl[c][name] = tile([P, PACK, CHUNKS[c][1]], F32, f"{name}{c}", REUSE[name, c])

        def first_two(c):
            late(c, "a")
            d = tl[c]
            j0, n = CHUNKS[c]
            for g in pairs:
                for t in range(g.start, g.stop):
                    nc.vector.tensor_copy(d["a"][:, t, :], y[t][:].indirect(entries(b1_t, j0, n)))
                for t in range(g.start, g.stop):
                    nc.vector.tensor_tensor(
                        d["p"][:, t, :], y[t][:].indirect(entries(b2_t, j0, n)), d["a"][:, t, :], ALU.subtract
                    )
                nc.scalar.activation(d["ap"][:, g, :], d["p"][:, g, :], ACT.Abs)

        def larger(c):
            d = tl[c]
            for g in pairs:
                nc.vector.scalar_tensor_tensor(d["nh"][:, g, :], d["p"][:, g, :], 0.0, d["a"][:, g, :], ALU.min, ALU.add)

        def third(c):
            late(c, "w")
            d = tl[c]
            j0, n = CHUNKS[c]
            for t in range(PACK):
                nc.vector.tensor_tensor(
                    d["w"][:, t, :], y[t][:].indirect(entries(b3_t, j0, n)), d["nh"][:, t, :], ALU.subtract
                )

        def signed_gain(c):
            late(c, "u")
            d = tl[c]
            for g in pairs:
                nc.vector.tensor_tensor(d["u"][:, g, :], d["w"][:, g, :], d["ap"][:, g, :], ALU.min)

        def price_turned(c):
            d = tl[c]
            n = CHUNKS[c][1]
            per_bank = 512 // n
            groups = [slice(t0, t0 + per_bank) for t0 in range(0, PACK, per_bank)]
            for g in pairs:
                nc.scalar.activation(d["ru"][:, g, :], d["u"][:, g, :], ACT.Relu)
            turned = []
            for g in groups:
                bank = psum.tile([P, 512], F32, name="bank")
                terms = [d[name][:, g, :].rearrange("p t j -> p (t j)") for name in ("nh", "ru")]
                for col in range(0, 512, P):
                    for i, term in enumerate(terms):
                        nc.tensor.matmul(
                            bank[:, col : col + P],
                            lhsT=term[:, col : col + P],
                            rhs=ident[:],
                            is_transpose=True,
                            start=i == 0,
                            stop=i == 1,
                        )
                s_t = tile([P, 512], F32, f"s_t{c}_{g.start}")
                nc.scalar.activation(s_t[:], bank[:], ACT.Sigmoid, scale=-1.0)
                turned.append(s_t)
            for g in pairs:
                nc.scalar.activation(d["au"][:, g, :], d["u"][:, g, :], ACT.Abs)
            d["s"] = []
            for s_t in turned:
                bank = psum.tile([P, 512], F32, name="bank")
                for col in range(0, 512, P):
                    nc.tensor.transpose(bank[:, col : col + P], s_t[:, col : col + P], ident[:])
                d["s"].extend(bank[:, i * n : (i + 1) * n] for i in range(per_bank))

        def price_direct(c):
            d = tl[c]
            n = CHUNKS[c][1]
            nmd = tile([P, PACK, n], F32, "nmd")
            s = [tile([P, 2, n], F32, f"s{gi}") for gi in range(2)]
            nc.scalar.activation(d["au"][:], d["u"][:], ACT.Abs)
            for gi, g in enumerate(pairs):
                nc.vector.scalar_tensor_tensor(nmd[:, g, :], d["u"][:, g, :], 0.0, d["nh"][:, g, :], ALU.max, ALU.add)
                nc.scalar.activation(s[gi][:], nmd[:, g, :], ACT.Sigmoid, scale=-1.0)
            d["s"] = [s[t // 2][:, t % 2, :] for t in range(PACK)]

        def gain(c):
            d = tl[c]
            for t in range(PACK):
                nc.vector.scalar_tensor_tensor(
                    d["z"][:, t, :], d["au"][:, t, :], gs_t[:, t : t + 1], d["s"][t], ALU.mult, ALU.mult
                )

        def weave(c):
            d = tl[c]
            src = d["z"][:].rearrange("p t j -> p j t")
            if c == last:
                for cols in (slice(0, 64), slice(64, 128)):
                    nc.vector.tensor_copy(d["zb"][:, cols, :], src[:, cols, :])
            elif c > 0:
                nc.vector.tensor_copy(d["zb"][:], src)
            else:
                nc.scalar.copy(d["zb"][:], src)

        def product(c):
            d = tl[c]
            j0, n = CHUNKS[c]
            d["zq"] = tile([P, n], U32, f"zq{c}", "s0" if c == last - 1 else None)
            for cols in (slice(0, 64), slice(64, 128)) if c == last else (slice(0, n),):
                nc.vector.quantize_mx(
                    out=d["zq"][:, cols].bitcast(FP8X4),
                    scales=d["zs"][:, cols],
                    in_=d["zb"][:, cols, :].rearrange("p j t -> p (j t)"),
                )
            for gi, g in enumerate(pairs):
                bank = psum.tile([P, 512], F32, name="bank")
                for e in range(2):
                    rows = slice((2 * gi + e) * P, (2 * gi + e + 1) * P)
                    nc.tensor.matmul_mx(
                        bank[:, e * n : (e + 1) * n],
                        lhsT=dw_pick[:, rows].bitcast(FP8X4),
                        lhsT_scale=ds_plane[:, rows],
                        rhs=d["zq"][:].bitcast(FP8X4),
                        rhs_scale=d["zs"][:],
                        start=True,
                        stop=True,
                    )
                dst = d["o"][:, g, :].rearrange("p a j -> p (a j)")
                if c == last and gi == 1:
                    nc.vector.tensor_scalar(dst, bank[:, : 2 * n], 0.0625, None, ALU.mult)
                else:
                    nc.scalar.activation(dst, bank[:, : 2 * n], ACT.Copy, scale=0.0625)
                queue = nc.scalar if c == last and gi == 0 else nc.sync
                queue.dma_start(
                    out[2 * gi * P : (2 * gi + 2) * P, j0 : j0 + n].rearrange("(a p) j -> p a j", p=P), d["o"][:, g, :]
                )

        first_two(0)
        larger(0)
        third(0)
        signed_gain(0)
        price_turned(0)
        first_two(1)
        larger(1)
        third(1)
        signed_gain(1)
        price_turned(1)
        gain(0)
        weave(0)
        first_two(2)
        larger(2)
        product(0)
        third(2)
        gain(1)
        signed_gain(2)
        price_direct(2)
        weave(1)
        gain(2)
        product(1)
        weave(2)
        product(2)
